import numpy as np
import ml_dtypes


def mxq(x, axis, fmt="e4m3"):
    dtype, down = {"e4m3": (ml_dtypes.float8_e4m3fn, 7), "e5m2": (ml_dtypes.float8_e5m2, 14)}[fmt]
    v = np.moveaxis(np.asarray(x, np.float32).astype(ml_dtypes.bfloat16).astype(np.float64), axis, -1)
    blocks = v.reshape(v.shape[:-1] + (-1, 32))
    amax = np.abs(blocks).max(-1, keepdims=True)
    byte = np.maximum(np.where(amax > 0, np.frexp(amax)[1] - 1 + 127, 0) - down, 1)
    scale = np.exp2(byte - 127.0)
    codes = (blocks / scale).astype(np.float32).astype(dtype).astype(np.float64)
    return np.moveaxis((codes * scale).reshape(v.shape), -1, axis)


WIDE = False


def mx_kscale(k):
    if not WIDE:
        return np.ones(k)
    levels = np.array([10, -10, 5, -5, 0])
    if k % 512:
        return np.exp2(np.random.permutation(np.resize(levels, k // 32))).repeat(32)
    a = np.empty((k // 512, 16))
    for p in range(k // 512):
        a[p, :8] = np.random.permutation(np.resize(levels, 8))
        for g in range(8):
            far = levels[np.abs(levels - a[p, g]) >= 10]
            a[p, g + 8] = far[np.random.randint(len(far))]
    return np.exp2(a.ravel()).repeat(32)


def f64(x):
    return np.asarray(x).astype(np.float64)


def striped(idx):
    return np.tile(np.asarray(idx).reshape(-1, 16).T, (8, 1)).astype(np.uint16)


def unstriped(offs):
    return offs[:16].T.reshape(-1).astype(np.int64)


E2M1 = np.array([0.0, 0.5, 1.0, 1.5, 2.0, 3.0, 4.0, 6.0, -0.0, -0.5, -1.0, -1.5, -2.0, -3.0, -4.0, -6.0])


def pack_weight(w, fmt):
    k, n = w.shape
    w = f64(np.asarray(w, np.float32).astype(ml_dtypes.bfloat16)).reshape(k // 32, 32, n)
    amax = np.abs(w).max(1)
    if fmt == "e4m3":
        byte = np.frexp(amax)[1] - 1 + 127 - 7
    else:
        mant, ex = np.frexp(amax / 6.0)
        byte = np.where(mant > 0.5, ex, ex - 1) + 127
    byte = np.clip(np.where(amax > 0, byte, 1), 1, 254)
    scaled = (w * np.exp2(127.0 - byte)[:, None, :]).reshape(k, n).astype(np.float32)
    by_word = np.ascontiguousarray(scaled.reshape(k // 512, 128, 4, n).transpose(0, 1, 3, 2))
    if fmt == "e4m3":
        words = by_word.astype(ml_dtypes.float8_e4m3fn).view(np.uint8)
    else:
        c = by_word.astype(ml_dtypes.float4_e2m1fn).view(np.uint8) & 0xF
        words = (c[..., 0::2] | (c[..., 1::2] << 4)).reshape(k // 512, 128, 2 * n)
    return np.ascontiguousarray(words), np.ascontiguousarray(byte.astype(np.uint8).reshape(k // 512, 16, n))


def unpack_weight(words, scales, fmt):
    g, _, n = scales.shape
    words = np.ascontiguousarray(words).reshape(g, 128, n, -1)
    if fmt == "e4m3":
        vals = words.view(ml_dtypes.float8_e4m3fn).astype(np.float64)
    else:
        nib = np.empty((g, 128, n, 4), np.uint8)
        nib[..., 0::2] = words & 0xF
        nib[..., 1::2] = words >> 4
        vals = E2M1[nib]
    vals = vals * np.repeat(np.exp2(scales.astype(np.float64) - 127.0), 8, axis=1)[..., None]
    return vals.transpose(0, 1, 3, 2).reshape(g * 512, n)


D, T, I, Q, E = 512, 2048, 512, 128, 512


def setup_inputs():
    n = np.random.standard_normal
    idx = np.random.permutation(T)[:I]
    fd = mx_kscale(D)
    fi = mx_kscale(I)
    ti = np.ones(T)
    ti[idx] = fi
    keysp = pack_weight(n((D, T)) / fd[:, None], "e2m1")
    return {
        "query": (n((D, Q)) * 0.25 / np.sqrt(D) * fd[:, None]).astype(np.float32),
        "keys_words": keysp[0],
        "keys_scales": keysp[1],
        "size": (np.random.uniform(0.5, 2.0, (1, I)) * fi).astype(np.float32),
        "vals": (n((E, T)) / ti).astype(np.float32),
        "gain": (np.random.uniform(0.5, 1.5, (1, E))).astype(np.float32),
        "gate": (np.random.uniform(0.3, 1.2, (Q, 1))).astype(np.float32),
        "res": (n((Q, E)) * 1.0).astype(np.float32),
        "offs": striped(idx),
    }


def reference(query, keys_words, keys_scales, size, vals, gain, gate, res, offs):
    idx = unstriped(offs)
    keysu = unpack_weight(keys_words, keys_scales, "e2m1")
    queryq = mxq(f64(query), 0, "e4m3")
    keysidxg = keysu[:, idx]
    a = queryq.T @ keysidxg
    p = np.exp(a - np.max(a, axis=1, keepdims=True))
    w = p * f64(size) / np.sum(p, axis=1, keepdims=True)
    wt = w.T
    vt = f64(vals)[:, idx].T
    wtq = mxq(wt, 0, "e4m3")
    vtq = mxq(vt, 0, "e4m3")
    o = wtq.T @ vtq
    nr = f64(gate) / np.sqrt(np.mean(np.square(o), axis=1, keepdims=True) + 0.0001)
    y = o * nr * f64(gain) + f64(res)
    return y

@@ -1,0 +1,191 @@
+from contextlib import ExitStack
+
+import concourse.mybir as mybir
+from concourse.masks import make_identity
+
+D, T, I, Q, E = 512, 2048, 512, 128, 512
+EPS = 0.0001
+FLOPS = 2 * Q * I * D + 2 * Q * E * I
+
+F32 = mybir.dt.float32
+BF16 = mybir.dt.bfloat16
+I32 = mybir.dt.int32
+U32 = mybir.dt.uint32
+U16 = mybir.dt.uint16
+U8 = mybir.dt.uint8
+FP8X4 = mybir.dt.float8_e4m3fn_x4
+FP4X4 = mybir.dt.float4_e2m1fn_x4
+ACT = mybir.ActivationFunctionType
+ALU = mybir.AluOpType
+AXIS = mybir.AxisListType
+
+P = 128
+PACK = 4
+BLOCKS = E // P
+EARLY = (BLOCKS - 1) * P
+
+
+def tile_attend_readscaled_kernel(tc, query, keys_words, keys_scales, size, vals, gain, gate, res, offs, out):
+    nc = tc.nc
+    with ExitStack() as ctx:
+        sb = ctx.enter_context(tc.tile_pool(name="sb", bufs=1))
+        ps = ctx.enter_context(tc.psum_pool(name="ps", bufs=1))
+        ps2 = ctx.enter_context(tc.psum_pool(name="ps2", bufs=2))
+
+        offsets = sb.tile([P, I // 16], U16, name="offsets")
+        key_words = sb.tile([P, T], U16, name="key_words", align_bytes=64)
+        key_scales = sb.tile([P, T], U8, name="key_scales", align_bytes=64)
+        query_raw = sb.tile([P, PACK, Q], F32, name="query_raw")
+        size_cols = sb.tile([P, PACK], F32, name="size_cols")
+        gain_cols = sb.tile([P, PACK], F32, name="gain_cols")
+        gate_col = sb.tile([P, 1], F32, name="gate_col")
+        res_sb = sb.tile([P, E], F32, name="res_sb")
+        pools = [sb.tile([P, T], F32, name=f"vals{b}", tag=f"vals{b}", align_bytes=64) for b in range(BLOCKS)]
+        ident = sb.tile([P, P], F32, name="ident")
+
+        nc.gpsimd.memset(key_scales[:].bitcast(I32), 0)
+        nc.sync.dma_start(offsets[:], offs)
+        nc.sync.dma_start(query_raw[:], query.rearrange("(p t) q -> p t q", t=PACK))
+        for r in range(4):
+            nc.sync.dma_start(key_scales[r:P:32, :].bitcast(I32), keys_scales[0, r:16:4, :].bitcast(I32))
+        nc.sync.dma_start(key_words[:].bitcast(I32), keys_words[0].bitcast(I32))
+        nc.sync.dma_start(pools[0][:], vals[0:P, :])
+        nc.sync.dma_start(size_cols[:], size.rearrange("o (p t) -> p (o t)", t=PACK))
+        nc.sync.dma_start(pools[1][:], vals[P : 2 * P, :])
+        nc.sync.dma_start(gain_cols[:], gain.rearrange("o (p t) -> p (o t)", t=PACK))
+        nc.sync.dma_start(gate_col[:], gate)
+        for b in range(2, BLOCKS):
+            nc.sync.dma_start(pools[b][:], vals[b * P : (b + 1) * P, :])
+        nc.sync.dma_start(res_sb[:], res)
+        make_identity(nc, ident[:])
+
+        def quantise(name, grouped, width, tag):
+            codes = sb.tile([P, width], U32, name=name + "_codes", tag=tag, align_bytes=64)
+            scales = sb.tile([P, width], U8, name=name + "_scales", align_bytes=64)
+            nc.vector.quantize_mx(out=codes[:].bitcast(FP8X4), scales=scales[:], in_=grouped)
+            return codes, scales
+
+        def turn(rows, grouped):
+            words = rows[:].bitcast(F32)
+            turned = ps2.tile([P, 2, P], F32, name="turned")
+            for u in range(2):
+                nc.tensor.transpose(turned[:, u, :], words[:, u : I // 2 : 2], ident[:])
+            nc.scalar.copy(
+                out=grouped.bitcast(F32).rearrange("p (c u) -> p c u", u=2),
+                in_=turned[:].rearrange("p u c -> p c u"),
+            )
+
+        def spread(name, cols):
+            rows = ps.tile([P, PACK, P], F32, name=name)
+            for t in range(PACK):
+                nc.tensor.transpose(rows[:, t, :], cols[:, t : t + 1].to_broadcast([P, P]), ident[:])
+            return rows[:].rearrange("q t s -> q s t")
+
+        def gather_vals(b):
+            picked = sb.tile([P, I], BF16, name=f"picked{b}", align_bytes=64)
+            nc.vector.tensor_copy(picked[:], pools[b][:].indirect(offsets[:]))
+            return picked
+
+        picked_words = sb.tile([P, I], U16, name="picked_words", align_bytes=64)
+        picked_scales = sb.tile([P, I], U8, name="picked_scales", align_bytes=64)
+        nc.vector.tensor_copy(picked_scales[:], key_scales[:].indirect(offsets[:]))
+        nc.vector.tensor_copy(picked_words[:], key_words[:].indirect(offsets[:]))
+
+        query_grouped = sb.tile([P, Q * PACK], BF16, name="query_grouped", align_bytes=64)
+        nc.scalar.copy(
+            out=query_grouped[:].rearrange("p (q t) -> p q t", t=PACK),
+            in_=query_raw[:].rearrange("p t q -> p q t"),
+        )
+        query_codes, query_scales = quantise("query", query_grouped[:], Q, "query_codes")
+
+        scores = ps.tile([P, I], F32, name="scores")
+        nc.tensor.matmul_mx(
+            out=scores[:],
+            lhsT=query_codes[:].bitcast(FP8X4),
+            lhsT_scale=query_scales[:],
+            rhs=picked_words[:].bitcast(FP4X4),
+            rhs_scale=picked_scales[:],
+            start=True,
+            stop=True,
+        )
+        size_rows = spread("size_rows", size_cols)
+        gain_rows = spread("gain_rows", gain_cols)
+
+        neg_max = sb.tile([P, 1], F32, name="neg_max")
+        nc.vector.tensor_reduce(neg_max[:], scores[:], AXIS.X, ALU.max, negate=True)
+        probs = sb.tile([P, I], F32, name="probs")
+        row_sum = sb.tile([P, 1], F32, name="row_sum")
+        nc.scalar.activation(probs[:], scores[:], ACT.Exp, bias=neg_max[:], accum_out=row_sum[:])
+        warm = sb.tile([P, 1], F32, name="warm")
+        nc.scalar.activation(warm[:], row_sum[:], ACT.Abs_reciprocal_sqrt)
+        picked = [gather_vals(0)]
+        inv_sum = sb.tile([P, 1], F32, name="inv_sum", tag="vals0", align_bytes=64)
+        nc.vector.reciprocal(inv_sum[:], row_sum[:])
+        weights = sb.tile([P, I], BF16, name="weights", align_bytes=64)
+        nc.vector.scalar_tensor_tensor(
+            out=weights[:].rearrange("q (s t) -> q s t", t=PACK),
+            in0=probs[:].rearrange("q (s t) -> q s t", t=PACK),
+            scalar=inv_sum[:],
+            in1=size_rows,
+            op0=ALU.mult,
+            op1=ALU.mult,
+        )
+        first = sb.tile([P, 2, I], BF16, name="first", align_bytes=64)
+        turn(picked[0], first[:, 1, :])
+        turn(weights, first[:, 0, :])
+        picked.append(gather_vals(1))
+        first_codes, first_scales = quantise("first", first[:].rearrange("p a c -> p (a c)"), 2 * P, "vals1")
+        weight_codes, weight_scales = first_codes[:, :P], first_scales[:, :P]
+
+        gain_gate = sb.tile([P, E], F32, name="gain_gate")
+        nc.scalar.activation(
+            gain_gate[:].rearrange("q (s t) -> q s t", t=PACK), gain_rows, ACT.Copy, scale=gate_col[:]
+        )
+
+        o_early = ps.tile([P, EARLY], F32, name="o_early")
+        o_last = ps.tile([P, P], F32, name="o_last")
+        for b in range(BLOCKS):
+            if b == 0:
+                codes, scales = first_codes[:, P:], first_scales[:, P:]
+            else:
+                grouped = sb.tile([P, I], BF16, name=f"grouped{b}", align_bytes=64)
+                turn(picked[b], grouped[:])
+                if b + 1 < BLOCKS:
+                    picked.append(gather_vals(b + 1))
+                codes, scales = quantise(f"val{b}", grouped[:], P, f"vals{b + 1}")
+                codes, scales = codes[:], scales[:]
+            nc.tensor.matmul_mx(
+                out=o_early[:, b * P : (b + 1) * P] if b < BLOCKS - 1 else o_last[:],
+                lhsT=weight_codes.bitcast(FP8X4),
+                lhsT_scale=weight_scales,
+                rhs=codes.bitcast(FP8X4),
+                rhs_scale=scales,
+                start=True,
+                stop=True,
+            )
+
+        squares = sb.tile([P, E], F32, name="squares")
+        sum_early = sb.tile([P, 1], F32, name="sum_early")
+        sum_last = sb.tile([P, 1], F32, name="sum_last")
+        mean_early = sb.tile([P, 1], F32, name="mean_early")
+        inv_rms = sb.tile([P, 1], F32, name="inv_rms")
+        scaled = sb.tile([P, E], F32, name="scaled")
+        nc.scalar.activation(squares[:, :EARLY], o_early[:], ACT.Square, accum_out=sum_early[:])
+        nc.scalar.activation(mean_early[:], sum_early[:], ACT.Copy, scale=1.0 / E, bias=EPS)
+        nc.vector.tensor_tensor(scaled[:, :EARLY], o_early[:], gain_gate[:, :EARLY], ALU.mult)
+        nc.scalar.activation(squares[:, EARLY:], o_last[:], ACT.Square, accum_out=sum_last[:])
+        nc.scalar.activation(inv_rms[:], sum_last[:], ACT.Abs_reciprocal_sqrt, scale=1.0 / E, bias=mean_early[:])
+        nc.vector.tensor_tensor(scaled[:, EARLY:], o_last[:], gain_gate[:, EARLY:], ALU.mult)
+
+        result = sb.tile([P, E], F32, name="result")
+        for h, queue in enumerate((nc.sync, nc.scalar)):
+            cols = slice(h * E // 2, (h + 1) * E // 2)
+            nc.vector.scalar_tensor_tensor(
+                out=result[:, cols],
+                in0=scaled[:, cols],
+                scalar=inv_rms[:],
+                in1=res_sb[:, cols],
+                op0=ALU.mult,
+                op1=ALU.add,
+            )
+            queue.dma_start(out[:, cols], result[:, cols])

@@ -45,10 +45,10 @@ def tile_attend_readscaled_kernel(tc, query, keys_words, keys_scales, size, vals
 
         nc.gpsimd.memset(key_scales[:].bitcast(I32), 0)
         nc.sync.dma_start(offsets[:], offs)
-        nc.sync.dma_start(query_raw[:], query.rearrange("(p t) q -> p t q", t=PACK))
+        nc.sync.dma_start(key_words[:].bitcast(I32), keys_words[0].bitcast(I32))
         for r in range(4):
             nc.sync.dma_start(key_scales[r:P:32, :].bitcast(I32), keys_scales[0, r:16:4, :].bitcast(I32))
-        nc.sync.dma_start(key_words[:].bitcast(I32), keys_words[0].bitcast(I32))
+        nc.sync.dma_start(query_raw[:], query.rearrange("(p t) q -> p t q", t=PACK))
         nc.sync.dma_start(pools[0][:], vals[0:P, :])
         nc.sync.dma_start(size_cols[:], size.rearrange("o (p t) -> p (o t)", t=PACK))
         nc.sync.dma_start(pools[1][:], vals[P : 2 * P, :])
@@ -64,6 +64,9 @@ def tile_attend_readscaled_kernel(tc, query, keys_words, keys_scales, size, vals
             scales = sb.tile([P, width], U8, name=name + "_scales", align_bytes=64)
             nc.vector.quantize_mx(out=codes[:].bitcast(FP8X4), scales=scales[:], in_=grouped)
             return codes, scales
+
+        def quantise_into(codes, scales, grouped):
+            nc.vector.quantize_mx(out=codes.bitcast(FP8X4), scales=scales, in_=grouped)
 
         def turn(rows, grouped):
             words = rows[:].bitcast(F32)
@@ -88,8 +91,8 @@ def tile_attend_readscaled_kernel(tc, query, keys_words, keys_scales, size, vals
 
         picked_words = sb.tile([P, I], U16, name="picked_words", align_bytes=64)
         picked_scales = sb.tile([P, I], U8, name="picked_scales", align_bytes=64)
-        nc.vector.tensor_copy(picked_scales[:], key_scales[:].indirect(offsets[:]))
         nc.vector.tensor_copy(picked_words[:], key_words[:].indirect(offsets[:]))
+        nc.vector.tensor_copy(picked_scales[:], key_scales[:].indirect(offsets[:]))
 
         query_grouped = sb.tile([P, Q * PACK], BF16, name="query_grouped", align_bytes=64)
         nc.scalar.copy(
@@ -118,8 +121,8 @@ def tile_attend_readscaled_kernel(tc, query, keys_words, keys_scales, size, vals
         nc.scalar.activation(probs[:], scores[:], ACT.Exp, bias=neg_max[:], accum_out=row_sum[:])
         warm = sb.tile([P, 1], F32, name="warm")
         nc.scalar.activation(warm[:], row_sum[:], ACT.Abs_reciprocal_sqrt)
-        picked = [gather_vals(0)]
-        inv_sum = sb.tile([P, 1], F32, name="inv_sum", tag="vals0", align_bytes=64)
+        picked = [gather_vals(0), gather_vals(1)]
+        inv_sum = sb.tile([P, 1], F32, name="inv_sum", tag="vals1", align_bytes=64)
         nc.vector.reciprocal(inv_sum[:], row_sum[:])
         weights = sb.tile([P, I], BF16, name="weights", align_bytes=64)
         nc.vector.scalar_tensor_tensor(
@@ -130,12 +133,16 @@ def tile_attend_readscaled_kernel(tc, query, keys_words, keys_scales, size, vals
             op0=ALU.mult,
             op1=ALU.mult,
         )
-        first = sb.tile([P, 2, I], BF16, name="first", align_bytes=64)
-        turn(picked[0], first[:, 1, :])
-        turn(weights, first[:, 0, :])
-        picked.append(gather_vals(1))
-        first_codes, first_scales = quantise("first", first[:].rearrange("p a c -> p (a c)"), 2 * P, "vals1")
-        weight_codes, weight_scales = first_codes[:, :P], first_scales[:, :P]
+        pair_grouped = sb.tile([P, 2, I], BF16, name="pair_grouped", align_bytes=64)
+        weight_grouped = sb.tile([P, I], BF16, name="weight_grouped", align_bytes=64)
+        turn(picked[0], pair_grouped[:, 0, :])
+        turn(picked[1], pair_grouped[:, 1, :])
+        turn(weights, weight_grouped[:])
+        picked.append(gather_vals(2))
+        first_codes = sb.tile([P, 3 * P], U32, name="first_codes", tag="vals2", align_bytes=64)
+        first_scales = sb.tile([P, 3 * P], U8, name="first_scales", align_bytes=64)
+        quantise_into(first_codes[:, P:], first_scales[:, P:], pair_grouped[:].rearrange("p a c -> p (a c)"))
+        quantise_into(first_codes[:, :P], first_scales[:, :P], weight_grouped[:])
 
         gain_gate = sb.tile([P, E], F32, name="gain_gate")
         nc.scalar.activation(
@@ -144,25 +151,28 @@ def tile_attend_readscaled_kernel(tc, query, keys_words, keys_scales, size, vals
 
         o_early = ps.tile([P, EARLY], F32, name="o_early")
         o_last = ps.tile([P, P], F32, name="o_last")
-        for b in range(BLOCKS):
-            if b == 0:
-                codes, scales = first_codes[:, P:], first_scales[:, P:]
-            else:
-                grouped = sb.tile([P, I], BF16, name=f"grouped{b}", align_bytes=64)
-                turn(picked[b], grouped[:])
-                if b + 1 < BLOCKS:
-                    picked.append(gather_vals(b + 1))
-                codes, scales = quantise(f"val{b}", grouped[:], P, f"vals{b + 1}")
-                codes, scales = codes[:], scales[:]
+
+        def read(acc, codes, scales):
             nc.tensor.matmul_mx(
-                out=o_early[:, b * P : (b + 1) * P] if b < BLOCKS - 1 else o_last[:],
-                lhsT=weight_codes.bitcast(FP8X4),
-                lhsT_scale=weight_scales,
+                out=acc,
+                lhsT=first_codes[:, :P].bitcast(FP8X4),
+                lhsT_scale=first_scales[:, :P],
                 rhs=codes.bitcast(FP8X4),
                 rhs_scale=scales,
                 start=True,
                 stop=True,
             )
+
+        read(o_early[:, : 2 * P], first_codes[:, P:], first_scales[:, P:])
+        grouped2 = sb.tile([P, I], BF16, name="grouped2", align_bytes=64)
+        turn(picked[2], grouped2[:])
+        picked.append(gather_vals(3))
+        grouped3 = sb.tile([P, I], BF16, name="grouped3", align_bytes=64)
+        turn(picked[3], grouped3[:])
+        codes2, scales2 = quantise("val2", grouped2[:], P, "vals3")
+        read(o_early[:, 2 * P :], codes2[:], scales2[:])
+        codes3, scales3 = quantise("val3", grouped3[:], P, "val3_codes")
+        read(o_last[:], codes3[:], scales3[:])
 
         squares = sb.tile([P, E], F32, name="squares")
         sum_early = sb.tile([P, 1], F32, name="sum_early")

from contextlib import ExitStack

import concourse.mybir as mybir
from concourse.masks import make_identity

D, T, I, Q, E = 512, 2048, 512, 128, 512
EPS = 0.0001
FLOPS = 2 * Q * I * D + 2 * Q * E * I

F32 = mybir.dt.float32
BF16 = mybir.dt.bfloat16
I32 = mybir.dt.int32
U32 = mybir.dt.uint32
U16 = mybir.dt.uint16
U8 = mybir.dt.uint8
FP8X4 = mybir.dt.float8_e4m3fn_x4
FP4X4 = mybir.dt.float4_e2m1fn_x4
ACT = mybir.ActivationFunctionType
ALU = mybir.AluOpType
AXIS = mybir.AxisListType

P = 128
PACK = 4
BLOCKS = E // P
EARLY = (BLOCKS - 1) * P


def tile_attend_readscaled_kernel(tc, query, keys_words, keys_scales, size, vals, gain, gate, res, offs, out):
    nc = tc.nc
    with ExitStack() as ctx:
        sb = ctx.enter_context(tc.tile_pool(name="sb", bufs=1))
        ps = ctx.enter_context(tc.psum_pool(name="ps", bufs=1))
        ps2 = ctx.enter_context(tc.psum_pool(name="ps2", bufs=2))

        offsets = sb.tile([P, I // 16], U16, name="offsets")
        key_words = sb.tile([P, T], U16, name="key_words", align_bytes=64)
        key_scales = sb.tile([P, T], U8, name="key_scales", align_bytes=64)
        query_raw = sb.tile([P, PACK, Q], F32, name="query_raw")
        size_cols = sb.tile([P, PACK], F32, name="size_cols")
        gain_cols = sb.tile([P, PACK], F32, name="gain_cols")
        gate_col = sb.tile([P, 1], F32, name="gate_col")
        res_sb = sb.tile([P, E], F32, name="res_sb")
        pools = [sb.tile([P, T], F32, name=f"vals{b}", tag=f"vals{b}", align_bytes=64) for b in range(BLOCKS)]
        ident = sb.tile([P, P], F32, name="ident")

        nc.gpsimd.memset(key_scales[:].bitcast(I32), 0)
        nc.sync.dma_start(offsets[:], offs)
        nc.sync.dma_start(key_words[:].bitcast(I32), keys_words[0].bitcast(I32))
        for r in range(4):
            nc.sync.dma_start(key_scales[r:P:32, :].bitcast(I32), keys_scales[0, r:16:4, :].bitcast(I32))
        nc.sync.dma_start(query_raw[:], query.rearrange("(p t) q -> p t q", t=PACK))
        nc.sync.dma_start(pools[0][:], vals[0:P, :])
        nc.sync.dma_start(size_cols[:], size.rearrange("o (p t) -> p (o t)", t=PACK))
        nc.sync.dma_start(pools[1][:], vals[P : 2 * P, :])
        nc.sync.dma_start(gain_cols[:], gain.rearrange("o (p t) -> p (o t)", t=PACK))
        nc.sync.dma_start(gate_col[:], gate)
        for b in range(2, BLOCKS):
            nc.sync.dma_start(pools[b][:], vals[b * P : (b + 1) * P, :])
        nc.sync.dma_start(res_sb[:], res)
        make_identity(nc, ident[:])

        def quantise(name, grouped, width, tag):
            codes = sb.tile([P, width], U32, name=name + "_codes", tag=tag, align_bytes=64)
            scales = sb.tile([P, width], U8, name=name + "_scales", align_bytes=64)
            nc.vector.quantize_mx(out=codes[:].bitcast(FP8X4), scales=scales[:], in_=grouped)
            return codes, scales

        def quantise_into(codes, scales, grouped):
            nc.vector.quantize_mx(out=codes.bitcast(FP8X4), scales=scales, in_=grouped)

        def turn(rows, grouped):
            words = rows[:].bitcast(F32)
            turned = ps2.tile([P, 2, P], F32, name="turned")
            for u in range(2):
                nc.tensor.transpose(turned[:, u, :], words[:, u : I // 2 : 2], ident[:])
            nc.scalar.copy(
                out=grouped.bitcast(F32).rearrange("p (c u) -> p c u", u=2),
                in_=turned[:].rearrange("p u c -> p c u"),
            )

        def spread(name, cols):
            rows = ps.tile([P, PACK, P], F32, name=name)
            for t in range(PACK):
                nc.tensor.transpose(rows[:, t, :], cols[:, t : t + 1].to_broadcast([P, P]), ident[:])
            return rows[:].rearrange("q t s -> q s t")

        def gather_vals(b):
            picked = sb.tile([P, I], BF16, name=f"picked{b}", align_bytes=64)
            nc.vector.tensor_copy(picked[:], pools[b][:].indirect(offsets[:]))
            return picked

        picked_words = sb.tile([P, I], U16, name="picked_words", align_bytes=64)
        picked_scales = sb.tile([P, I], U8, name="picked_scales", align_bytes=64)
        nc.vector.tensor_copy(picked_words[:], key_words[:].indirect(offsets[:]))
        nc.vector.tensor_copy(picked_scales[:], key_scales[:].indirect(offsets[:]))

        query_grouped = sb.tile([P, Q * PACK], BF16, name="query_grouped", align_bytes=64)
        nc.scalar.copy(
            out=query_grouped[:].rearrange("p (q t) -> p q t", t=PACK),
            in_=query_raw[:].rearrange("p t q -> p q t"),
        )
        query_codes, query_scales = quantise("query", query_grouped[:], Q, "query_codes")

        scores = ps.tile([P, I], F32, name="scores")
        nc.tensor.matmul_mx(
            out=scores[:],
            lhsT=query_codes[:].bitcast(FP8X4),
            lhsT_scale=query_scales[:],
            rhs=picked_words[:].bitcast(FP4X4),
            rhs_scale=picked_scales[:],
            start=True,
            stop=True,
        )
        size_rows = spread("size_rows", size_cols)
        gain_rows = spread("gain_rows", gain_cols)

        neg_max = sb.tile([P, 1], F32, name="neg_max")
        nc.vector.tensor_reduce(neg_max[:], scores[:], AXIS.X, ALU.max, negate=True)
        probs = sb.tile([P, I], F32, name="probs")
        row_sum = sb.tile([P, 1], F32, name="row_sum")
        nc.scalar.activation(probs[:], scores[:], ACT.Exp, bias=neg_max[:], accum_out=row_sum[:])
        warm = sb.tile([P, 1], F32, name="warm")
        nc.scalar.activation(warm[:], row_sum[:], ACT.Abs_reciprocal_sqrt)
        picked = [gather_vals(0), gather_vals(1)]
        inv_sum = sb.tile([P, 1], F32, name="inv_sum", tag="vals1", align_bytes=64)
        nc.vector.reciprocal(inv_sum[:], row_sum[:])
        weights = sb.tile([P, I], BF16, name="weights", align_bytes=64)
        nc.vector.scalar_tensor_tensor(
            out=weights[:].rearrange("q (s t) -> q s t", t=PACK),
            in0=probs[:].rearrange("q (s t) -> q s t", t=PACK),
            scalar=inv_sum[:],
            in1=size_rows,
            op0=ALU.mult,
            op1=ALU.mult,
        )
        pair_grouped = sb.tile([P, 2, I], BF16, name="pair_grouped", align_bytes=64)
        weight_grouped = sb.tile([P, I], BF16, name="weight_grouped", align_bytes=64)
        turn(picked[0], pair_grouped[:, 0, :])
        turn(picked[1], pair_grouped[:, 1, :])
        turn(weights, weight_grouped[:])
        picked.append(gather_vals(2))
        first_codes = sb.tile([P, 3 * P], U32, name="first_codes", tag="vals2", align_bytes=64)
        first_scales = sb.tile([P, 3 * P], U8, name="first_scales", align_bytes=64)
        quantise_into(first_codes[:, P:], first_scales[:, P:], pair_grouped[:].rearrange("p a c -> p (a c)"))
        quantise_into(first_codes[:, :P], first_scales[:, :P], weight_grouped[:])

        gain_gate = sb.tile([P, E], F32, name="gain_gate")
        nc.scalar.activation(
            gain_gate[:].rearrange("q (s t) -> q s t", t=PACK), gain_rows, ACT.Copy, scale=gate_col[:]
        )

        o_early = ps.tile([P, EARLY], F32, name="o_early")
        o_last = ps.tile([P, P], F32, name="o_last")

        def read(acc, codes, scales):
            nc.tensor.matmul_mx(
                out=acc,
                lhsT=first_codes[:, :P].bitcast(FP8X4),
                lhsT_scale=first_scales[:, :P],
                rhs=codes.bitcast(FP8X4),
                rhs_scale=scales,
                start=True,
                stop=True,
            )

        read(o_early[:, : 2 * P], first_codes[:, P:], first_scales[:, P:])
        grouped2 = sb.tile([P, I], BF16, name="grouped2", align_bytes=64)
        turn(picked[2], grouped2[:])
        picked.append(gather_vals(3))
        grouped3 = sb.tile([P, I], BF16, name="grouped3", align_bytes=64)
        turn(picked[3], grouped3[:])
        codes2, scales2 = quantise("val2", grouped2[:], P, "vals3")
        read(o_early[:, 2 * P :], codes2[:], scales2[:])
        codes3, scales3 = quantise("val3", grouped3[:], P, "val3_codes")
        read(o_last[:], codes3[:], scales3[:])

        squares = sb.tile([P, E], F32, name="squares")
        sum_early = sb.tile([P, 1], F32, name="sum_early")
        sum_last = sb.tile([P, 1], F32, name="sum_last")
        mean_early = sb.tile([P, 1], F32, name="mean_early")
        inv_rms = sb.tile([P, 1], F32, name="inv_rms")
        scaled = sb.tile([P, E], F32, name="scaled")
        nc.scalar.activation(squares[:, :EARLY], o_early[:], ACT.Square, accum_out=sum_early[:])
        nc.scalar.activation(mean_early[:], sum_early[:], ACT.Copy, scale=1.0 / E, bias=EPS)
        nc.vector.tensor_tensor(scaled[:, :EARLY], o_early[:], gain_gate[:, :EARLY], ALU.mult)
        nc.scalar.activation(squares[:, EARLY:], o_last[:], ACT.Square, accum_out=sum_last[:])
        nc.scalar.activation(inv_rms[:], sum_last[:], ACT.Abs_reciprocal_sqrt, scale=1.0 / E, bias=mean_early[:])
        nc.vector.tensor_tensor(scaled[:, EARLY:], o_last[:], gain_gate[:, EARLY:], ALU.mult)

        result = sb.tile([P, E], F32, name="result")
        for h, queue in enumerate((nc.sync, nc.scalar)):
            cols = slice(h * E // 2, (h + 1) * E // 2)
            nc.vector.scalar_tensor_tensor(
                out=result[:, cols],
                in0=scaled[:, cols],
                scalar=inv_rms[:],
                in1=res_sb[:, cols],
                op0=ALU.mult,
                op1=ALU.add,
            )
            queue.dma_start(out[:, cols], result[:, cols])
